import numpy as np
import ml_dtypes


def mxq(x, axis, fmt="e4m3"):
    dtype, down = {"e4m3": (ml_dtypes.float8_e4m3fn, 7), "e5m2": (ml_dtypes.float8_e5m2, 14)}[fmt]
    v = np.moveaxis(np.asarray(x, np.float32).astype(ml_dtypes.bfloat16).astype(np.float64), axis, -1)
    blocks = v.reshape(v.shape[:-1] + (-1, 32))
    amax = np.abs(blocks).max(-1, keepdims=True)
    byte = np.maximum(np.where(amax > 0, np.frexp(amax)[1] - 1 + 127, 0) - down, 1)
    scale = np.exp2(byte - 127.0)
    codes = (blocks / scale).astype(np.float32).astype(dtype).astype(np.float64)
    return np.moveaxis((codes * scale).reshape(v.shape), -1, axis)


WIDE = False


def mx_kscale(k):
    if not WIDE:
        return np.ones(k)
    levels = np.array([10, -10, 5, -5, 0])
    if k % 512:
        return np.exp2(np.random.permutation(np.resize(levels, k // 32))).repeat(32)
    a = np.empty((k // 512, 16))
    for p in range(k // 512):
        a[p, :8] = np.random.permutation(np.resize(levels, 8))
        for g in range(8):
            far = levels[np.abs(levels - a[p, g]) >= 10]
            a[p, g + 8] = far[np.random.randint(len(far))]
    return np.exp2(a.ravel()).repeat(32)


def f64(x):
    return np.asarray(x).astype(np.float64)


def striped(idx):
    return np.tile(idx.reshape(-1, 16).T, (8, 1)).astype(np.uint16)


def unstriped(offs):
    return offs[:16].T.reshape(-1).astype(np.int64)


def striped8(idx):
    return np.concatenate([x.reshape(-1, 16).T for x in idx]).astype(np.uint16)


def runs(offs, k):
    lists = np.stack([offs[16 * r : 16 * r + 16].T.reshape(-1) for r in range(8)]).astype(np.int64)
    return lists[np.arange(k) % 512 // 64]


def pack_weight(w):
    k, n = w.shape
    w = f64(np.asarray(w, np.float32).astype(ml_dtypes.bfloat16)).reshape(k // 32, 32, n)
    amax = np.abs(w).max(1)
    byte = np.clip(np.where(amax > 0, np.frexp(amax)[1] - 1 + 127 - 7, 1), 1, 254)
    scaled = (w * np.exp2(127.0 - byte)[:, None, :]).reshape(k, n).astype(np.float32)
    words = np.ascontiguousarray(scaled.reshape(k // 512, 128, 4, n).transpose(0, 1, 3, 2)).astype(ml_dtypes.float8_e4m3fn).view(np.uint8)
    return words, np.ascontiguousarray(byte.astype(np.uint8).reshape(k // 512, 16, n))


def unpack_weight(words, scales):
    g, p, n, _ = words.shape
    vals = np.ascontiguousarray(words).view(ml_dtypes.float8_e4m3fn).astype(np.float64) * np.repeat(np.exp2(scales.astype(np.float64) - 127.0), 8, axis=1)[..., None]
    return vals.transpose(0, 1, 3, 2).reshape(g * 512, n)


K, T, S, G, H, W, C = 512, 1024, 256, 2048, 512, 128, 512


def setup_inputs():
    n = np.random.standard_normal
    s = mx_kscale(K)[:, None]
    packed_xT = pack_weight(n((K, T)) * s)
    packed_dT = pack_weight(n((K, G)) / s)
    perm = np.random.permutation(S)
    perm2 = np.random.permutation(S)
    return {
        "x_words": packed_xT[0],
        "x_scales": packed_xT[1],
        "d_words": packed_dT[0],
        "d_scales": packed_dT[1],
        "gs": (np.random.uniform(0.5, 1.5, (K, 1)) / s).astype(np.float32),
        "offs": striped8(np.random.randint(0, T, (8, S))),
        "k1": striped8(np.random.randint(0, G, (8, H))),
        "n1": striped(perm[:W]),
        "n2": striped(perm[W:]),
        "n3": striped(np.random.permutation(S)),
        "cand": striped8(np.random.randint(0, T, (8, C))),
        "n4": striped(perm2[:W]),
        "n5": striped(perm2[W:]),
        "n6": striped(np.random.permutation(S)),
    }


def reference(x_words, x_scales, d_words, d_scales, gs, offs, k1, n1, n2, n3, cand, n4, n5, n6):
    x_cand = unpack_weight(x_words, x_scales)[np.arange(K)[:, None], runs(cand, K)]
    d_k1 = unpack_weight(d_words, d_scales)[np.arange(K)[:, None], runs(k1, K)]
    xq = unpack_weight(x_words, x_scales)[np.arange(K)[:, None], runs(offs, K)]
    h = 0.0625 * (d_k1.T @ xq)
    pa = h[:, unstriped(n1)]
    pb = h[:, unstriped(n2)]
    rb = np.minimum(pa, pb)
    ra = np.maximum(pa, pb)
    ds = np.zeros((H, S))
    ds[:, unstriped(n1)] = ra
    dt = ds.copy()
    dt[:, unstriped(n2)] = rb
    z = f64(gs) * (dt - dt[:, unstriped(n3)])
    s = 0.0625 * ((x_cand.T @ mxq(z, 0, "e4m3")))
    pa2 = s[:, unstriped(n4)]
    pb2 = s[:, unstriped(n5)]
    rb2 = pa2 - pb2
    ds2 = np.zeros((C, S))
    ds2[:, unstriped(n4)] = pb2
    dt2 = ds2.copy()
    dt2[:, unstriped(n5)] = rb2
    return np.maximum(dt2, 0.5 * dt2[:, unstriped(n6)])

@@ -1,0 +1,218 @@
+from contextlib import ExitStack
+
+import concourse.mybir as mybir
+
+K, T, S, G, H, W, C = 512, 1024, 256, 2048, 512, 128, 512
+FLOPS = 2 * K * H * S + 2 * K * C * S
+
+F32 = mybir.dt.float32
+BF16 = mybir.dt.bfloat16
+I32 = mybir.dt.int32
+U32 = mybir.dt.uint32
+U16 = mybir.dt.uint16
+U8 = mybir.dt.uint8
+FP8X4 = mybir.dt.float8_e4m3fn_x4
+ALU = mybir.AluOpType
+COPY = mybir.ActivationFunctionType.Copy
+
+P = 128
+PACK = 4
+GROUP = 16
+QUAD = 32
+BLOCK = 8
+WIDE = S + 8
+HALVES = ((0, 128), (128, 256))
+LAST_PIECES = ((0, 64), (64, 128), (128, 256))
+
+
+def tile_picked_hpqhorddswapd_none_p_kernel(
+    tc, x_words, x_scales, d_words, d_scales, gs, offs, k1, n1, n2, n3, cand, n4, n5, n6, out
+):
+    nc = tc.nc
+    with ExitStack() as ctx:
+        lists = ctx.enter_context(tc.tile_pool(name="lists", bufs=1))
+        keep = ctx.enter_context(tc.tile_pool(name="keep", bufs=1))
+        psum = ctx.enter_context(tc.psum_pool(name="psum", bufs=1))
+
+        def load_list(name, source):
+            held = lists.tile([P, source.shape[1]], U16, name=name)
+            nc.sync.dma_start(held[:], source)
+            return held
+
+        def load_scale_table(name, source):
+            table = keep.tile([P, source.shape[2]], U8, name=name, align_bytes=64)
+            rows = source[0].bitcast(I32)
+            spread = rows.unsqueeze(1).to_broadcast([rows.shape[0], BLOCK, rows.shape[1]])
+            nc.sync.dma_start(table[:].bitcast(I32), spread)
+            return table
+
+        def load_word_table(name, source):
+            table = keep.tile([P, source.shape[2]], U32, name=name, align_bytes=64)
+            nc.sync.dma_start(table[:].bitcast(I32), source[0].rearrange("p n t -> p (n t)").bitcast(I32))
+            return table
+
+        def place_rows(plane, queue):
+            for i in range(1, QUAD // BLOCK):
+                queue.dma_start(plane[i:P:QUAD, :].bitcast(I32), plane[BLOCK * i : P : QUAD, :].bitcast(I32))
+
+        k1_l = load_list("k1_l", k1)
+        d_sc = load_scale_table("d_sc", d_scales)
+        offs_l = load_list("offs_l", offs)
+        x_sc = load_scale_table("x_sc", x_scales)
+        n1_l = load_list("n1_l", n1)
+        n2_l = load_list("n2_l", n2)
+        n3_l = load_list("n3_l", n3)
+        d_w = load_word_table("d_w", d_words)
+        x_w = load_word_table("x_w", x_words)
+        cand_l = load_list("cand_l", cand)
+        n4_l = load_list("n4_l", n4)
+        n5_l = load_list("n5_l", n5)
+        n6_l = load_list("n6_l", n6)
+
+        first_sc = keep.tile([P, H + S], U8, name="first_sc", align_bytes=64)
+        nc.vector.tensor_copy(first_sc[:, :H], d_sc[:].indirect(k1_l[:]))
+        nc.vector.tensor_copy(first_sc[:, H:], x_sc[:].indirect(offs_l[:]))
+        first_plane = keep.tile([P, H + S], U8, name="first_plane", align_bytes=64)
+        nc.vector.tensor_copy(
+            first_plane[:, :H].rearrange("p (t m) -> p t m", t=PACK),
+            first_sc[:, :H].rearrange("p (m t) -> p t m", t=PACK),
+        )
+        nc.vector.tensor_copy(first_plane[:, H:].bitcast(I32), first_sc[:, H:].bitcast(I32))
+        place_rows(first_plane, nc.scalar)
+        dk_w = keep.tile([P, H], U32, name="dk_w", align_bytes=64)
+        nc.vector.tensor_copy(dk_w[:], d_w[:].indirect(k1_l[:]))
+        xq_w = keep.tile([P, S], U32, name="xq_w", align_bytes=64)
+        nc.vector.tensor_copy(xq_w[:], x_w[:].indirect(offs_l[:]))
+
+        h = []
+        for t in range(PACK):
+            dealt_w = keep.tile([P, P], U32, name="dealt_w%d" % t, align_bytes=64)
+            nc.vector.tensor_copy(dealt_w[:], dk_w[:, t:H:PACK])
+            acc = psum.tile([P, S], F32, name="acc_h%d" % t, tag="bank%d" % t)
+            nc.tensor.matmul_mx(
+                out=acc[:],
+                lhsT=dealt_w[:].bitcast(FP8X4),
+                lhsT_scale=first_plane[:, t * P : (t + 1) * P],
+                rhs=xq_w[:].bitcast(FP8X4),
+                rhs_scale=first_plane[:, H:],
+                start=True,
+                stop=True,
+            )
+            h_t = keep.tile([P, S], F32, name="h%d" % t)
+            nc.vector.tensor_scalar(h_t[:], acc[:], 0.0625, None, ALU.mult)
+            h.append(h_t)
+
+        gain = keep.tile([P, PACK], F32, name="gain", tag="d_w", align_bytes=64)
+        nc.sync.dma_start(gain[:], gs.rearrange("(p t) o -> p (t o)", t=PACK))
+
+        def fetch(name, window, offsets, tag=None):
+            got = keep.tile([P, offsets.shape[1] * GROUP], F32, name=name, tag=tag or name, align_bytes=64)
+            nc.scalar.activation(got[:], window[:].indirect(offsets), COPY)
+            return got
+
+        def put(window, offsets, values):
+            nc.scalar.activation(window[:].indirect(offsets), values, COPY)
+
+        z = keep.tile([P, S, PACK], BF16, name="z", align_bytes=64)
+        z_w = keep.tile([P, S], U32, name="z_w", align_bytes=64)
+        z_sc = keep.tile([P, S], U8, name="z_sc", align_bytes=64)
+        pa, pb, weighted, dt, xc_w = {}, {}, {}, {}, {}
+        held = {}
+
+        def fetch_a(t):
+            pa[t] = fetch("pa%d" % t, h[t], n1_l[:], "slot_a%d" % t)
+
+        def fetch_b(t):
+            pb[t] = fetch("pb%d" % t, h[t], n2_l[:], "slot_b%d" % t)
+            pair = keep.tile([P, 2 * W], F32, name="pair%d" % t)
+            nc.vector.tensor_tensor(pair[:, :W], pa[t][:], pb[t][:], ALU.max)
+            nc.vector.tensor_tensor(pair[:, W:], pa[t][:], pb[t][:], ALU.min)
+            weighted[t] = keep.tile([P, 2 * W], F32, name="weighted%d" % t)
+            nc.vector.tensor_scalar(weighted[t][:], pair[:], gain[:, t : t + 1], None, ALU.mult)
+            if t == 0:
+                cand_sc = keep.tile([P, C], U8, name="cand_sc", tag="slot_b0", align_bytes=64)
+                nc.vector.tensor_copy(cand_sc[:], x_sc[:].indirect(cand_l[:]))
+                held["cand_plane"] = keep.tile([P, C], U8, name="cand_plane", align_bytes=64)
+                nc.vector.tensor_copy(held["cand_plane"][:].bitcast(I32), cand_sc[:].bitcast(I32))
+                place_rows(held["cand_plane"], nc.sync)
+            xc_w[t] = keep.tile([P, P], U32, name="xc_w%d" % t, tag="slot_a%d" % t, align_bytes=64)
+            nc.vector.tensor_copy(xc_w[t][:], x_w[:].indirect(cand_l[:, t * P // GROUP : (t + 1) * P // GROUP]))
+
+        def put_a(t):
+            dt[t] = keep.tile([P, WIDE], F32, name="dt%d" % t)
+            put(dt[t], n1_l[:], weighted[t][:, :W])
+
+        def put_b(t):
+            put(dt[t], n2_l[:], weighted[t][:, W:])
+
+        def finish_z(t, lo, hi):
+            other = fetch("dt_n3_%d_%d" % (t, lo), dt[t], n3_l[:, lo // GROUP : hi // GROUP])
+            nc.vector.tensor_tensor(z[:, lo:hi, t], dt[t][:, lo:hi], other[:], ALU.subtract)
+            if t == PACK - 1 and hi % (S // 2) == 0:
+                lo = hi - S // 2
+                nc.vector.quantize_mx(
+                    out=z_w[:, lo:hi].bitcast(FP8X4),
+                    scales=z_sc[:, lo:hi],
+                    in_=z[:, lo:hi, :].rearrange("p n t -> p (n t)"),
+                )
+
+        def weave(get_a, get_b, set_a, set_b, finish, before, pieces):
+            for b in range(3):
+                get_a(b)
+                get_b(b)
+            set_a(0)
+            get_a(3)
+            set_b(0)
+            get_b(3)
+            for b in range(1, 4):
+                set_a(b)
+                finish(b - 1, 0, S if b < 3 else before)
+                set_b(b)
+            if before < S:
+                finish(2, before, S)
+            for lo, hi in pieces:
+                finish(3, lo, hi)
+
+        weave(fetch_a, fetch_b, put_a, put_b, finish_z, S, LAST_PIECES)
+
+        s = []
+        for c in range(C // P):
+            s_c = keep.tile([P, S], F32, name="s%d" % c)
+            for i, (lo, hi) in enumerate(HALVES if c == 0 else ((0, S),)):
+                acc = psum.tile([P, hi - lo], F32, name="acc_s%d_%d" % (c, i), tag="bank%d" % ((PACK + c + 4 * i) % 8))
+                nc.tensor.matmul_mx(
+                    out=acc[:],
+                    lhsT=xc_w[c][:].bitcast(FP8X4),
+                    lhsT_scale=held["cand_plane"][:, c * P : (c + 1) * P],
+                    rhs=z_w[:, lo:hi].bitcast(FP8X4),
+                    rhs_scale=z_sc[:, lo:hi],
+                    start=True,
+                    stop=True,
+                )
+                nc.vector.tensor_scalar(s_c[:, lo:hi], acc[:], 0.0625, None, ALU.mult)
+            s.append(s_c)
+
+        pa2, pb2, rb2, dt2 = {}, {}, {}, {}
+
+        def fetch_a2(c):
+            pa2[c] = fetch("pa2_%d" % c, s[c], n4_l[:])
+
+        def fetch_b2(c):
+            pb2[c] = fetch("pb2_%d" % c, s[c], n5_l[:])
+            rb2[c] = keep.tile([P, W], F32, name="rb2_%d" % c)
+            nc.vector.tensor_tensor(rb2[c][:], pa2[c][:], pb2[c][:], ALU.subtract)
+
+        def put_a2(c):
+            dt2[c] = keep.tile([P, WIDE], F32, name="dt2_%d" % c)
+            put(dt2[c], n4_l[:], pb2[c][:])
+
+        def put_b2(c):
+            put(dt2[c], n5_l[:], rb2[c][:])
+
+        def finish_out(c, lo, hi):
+            other = fetch("dt2_n6_%d_%d" % (c, lo), dt2[c], n6_l[:, lo // GROUP : hi // GROUP])
+            result = keep.tile([P, hi - lo], F32, name="result%d_%d" % (c, lo))
+            nc.vector.scalar_tensor_tensor(result[:], other[:], 0.5, dt2[c][:, lo:hi], ALU.mult, ALU.max)
+            nc.sync.dma_start(out[c * P : (c + 1) * P, lo:hi], result[:])
+
+        weave(fetch_a2, fetch_b2, put_a2, put_b2, finish_out, S // 2, HALVES)

@@ -43,7 +43,7 @@ def tile_picked_hpqhorddswapd_none_p_kernel(
             table = keep.tile([P, source.shape[2]], U8, name=name, align_bytes=64)
             rows = source[0].bitcast(I32)
             spread = rows.unsqueeze(1).to_broadcast([rows.shape[0], BLOCK, rows.shape[1]])
-            nc.sync.dma_start(table[:].bitcast(I32), spread)
+            nc.scalar.dma_start(table[:].bitcast(I32), spread)
             return table
 
         def load_word_table(name, source):
@@ -51,14 +51,14 @@ def tile_picked_hpqhorddswapd_none_p_kernel(
             nc.sync.dma_start(table[:].bitcast(I32), source[0].rearrange("p n t -> p (n t)").bitcast(I32))
             return table
 
-        def place_rows(plane, queue):
+        def place_rows(plane, queues):
             for i in range(1, QUAD // BLOCK):
-                queue.dma_start(plane[i:P:QUAD, :].bitcast(I32), plane[BLOCK * i : P : QUAD, :].bitcast(I32))
+                queues[i - 1].dma_start(plane[i:P:QUAD, :].bitcast(I32), plane[BLOCK * i : P : QUAD, :].bitcast(I32))
 
-        k1_l = load_list("k1_l", k1)
         d_sc = load_scale_table("d_sc", d_scales)
-        offs_l = load_list("offs_l", offs)
+        k1_l = load_list("k1_l", k1)
         x_sc = load_scale_table("x_sc", x_scales)
+        offs_l = load_list("offs_l", offs)
         n1_l = load_list("n1_l", n1)
         n2_l = load_list("n2_l", n2)
         n3_l = load_list("n3_l", n3)
@@ -70,36 +70,41 @@ def tile_picked_hpqhorddswapd_none_p_kernel(
         n6_l = load_list("n6_l", n6)
 
         first_sc = keep.tile([P, H + S], U8, name="first_sc", align_bytes=64)
+        first_plane = keep.tile([P, H + S], U8, name="first_plane", align_bytes=64)
         nc.vector.tensor_copy(first_sc[:, :H], d_sc[:].indirect(k1_l[:]))
         nc.vector.tensor_copy(first_sc[:, H:], x_sc[:].indirect(offs_l[:]))
-        first_plane = keep.tile([P, H + S], U8, name="first_plane", align_bytes=64)
         nc.vector.tensor_copy(
             first_plane[:, :H].rearrange("p (t m) -> p t m", t=PACK),
             first_sc[:, :H].rearrange("p (m t) -> p t m", t=PACK),
         )
         nc.vector.tensor_copy(first_plane[:, H:].bitcast(I32), first_sc[:, H:].bitcast(I32))
-        place_rows(first_plane, nc.scalar)
+        place_rows(first_plane, (nc.scalar, nc.scalar, nc.scalar))
         dk_w = keep.tile([P, H], U32, name="dk_w", align_bytes=64)
         nc.vector.tensor_copy(dk_w[:], d_w[:].indirect(k1_l[:]))
         xq_w = keep.tile([P, S], U32, name="xq_w", align_bytes=64)
-        nc.vector.tensor_copy(xq_w[:], x_w[:].indirect(offs_l[:]))
+        for lo, hi in HALVES:
+            nc.vector.tensor_copy(xq_w[:, lo:hi], x_w[:].indirect(offs_l[:, lo // GROUP : hi // GROUP]))
 
         h = []
         for t in range(PACK):
             dealt_w = keep.tile([P, P], U32, name="dealt_w%d" % t, align_bytes=64)
             nc.vector.tensor_copy(dealt_w[:], dk_w[:, t:H:PACK])
-            acc = psum.tile([P, S], F32, name="acc_h%d" % t, tag="bank%d" % t)
-            nc.tensor.matmul_mx(
-                out=acc[:],
-                lhsT=dealt_w[:].bitcast(FP8X4),
-                lhsT_scale=first_plane[:, t * P : (t + 1) * P],
-                rhs=xq_w[:].bitcast(FP8X4),
-                rhs_scale=first_plane[:, H:],
-                start=True,
-                stop=True,
-            )
             h_t = keep.tile([P, S], F32, name="h%d" % t)
-            nc.vector.tensor_scalar(h_t[:], acc[:], 0.0625, None, ALU.mult)
+            for i, (lo, hi) in enumerate(HALVES if t == 0 else ((0, S),)):
+                acc = psum.tile([P, hi - lo], F32, name="acc_h%d_%d" % (t, i), tag="bank%d" % (t + PACK * i))
+                nc.tensor.matmul_mx(
+                    out=acc[:],
+                    lhsT=dealt_w[:].bitcast(FP8X4),
+                    lhsT_scale=first_plane[:, t * P : (t + 1) * P],
+                    rhs=xq_w[:, lo:hi].bitcast(FP8X4),
+                    rhs_scale=first_plane[:, H + lo : H + hi],
+                    start=True,
+                    stop=True,
+                )
+                if t == 0 and i == 0:
+                    nc.scalar.activation(h_t[:, lo:hi], acc[:], COPY, scale=0.0625)
+                else:
+                    nc.vector.tensor_scalar(h_t[:, lo:hi], acc[:], 0.0625, None, ALU.mult)
             h.append(h_t)
 
         gain = keep.tile([P, PACK], F32, name="gain", tag="d_w", align_bytes=64)
@@ -116,37 +121,46 @@ def tile_picked_hpqhorddswapd_none_p_kernel(
         z = keep.tile([P, S, PACK], BF16, name="z", align_bytes=64)
         z_w = keep.tile([P, S], U32, name="z_w", align_bytes=64)
         z_sc = keep.tile([P, S], U8, name="z_sc", align_bytes=64)
-        pa, pb, weighted, dt, xc_w = {}, {}, {}, {}, {}
+        pa, pb, ra, rb, dt, xc_w = {}, {}, {}, {}, {}, {}
         held = {}
 
         def fetch_a(t):
-            pa[t] = fetch("pa%d" % t, h[t], n1_l[:], "slot_a%d" % t)
+            pa[t] = fetch("pa%d" % t, h[t], n1_l[:])
 
         def fetch_b(t):
             pb[t] = fetch("pb%d" % t, h[t], n2_l[:], "slot_b%d" % t)
-            pair = keep.tile([P, 2 * W], F32, name="pair%d" % t)
-            nc.vector.tensor_tensor(pair[:, :W], pa[t][:], pb[t][:], ALU.max)
-            nc.vector.tensor_tensor(pair[:, W:], pa[t][:], pb[t][:], ALU.min)
-            weighted[t] = keep.tile([P, 2 * W], F32, name="weighted%d" % t)
-            nc.vector.tensor_scalar(weighted[t][:], pair[:], gain[:, t : t + 1], None, ALU.mult)
-            if t == 0:
-                cand_sc = keep.tile([P, C], U8, name="cand_sc", tag="slot_b0", align_bytes=64)
+            high = keep.tile([P, W], F32, name="high%d" % t, align_bytes=64)
+            low = keep.tile([P, W], F32, name="low%d" % t, align_bytes=64)
+            ra[t] = keep.tile([P, W], F32, name="ra%d" % t, align_bytes=64)
+            rb[t] = keep.tile([P, W], F32, name="rb%d" % t, align_bytes=64)
+            nc.vector.tensor_tensor(high[:], pa[t][:], pb[t][:], ALU.max)
+            nc.vector.tensor_tensor(low[:], pa[t][:], pb[t][:], ALU.min)
+            nc.vector.tensor_scalar(ra[t][:], high[:], gain[:, t : t + 1], None, ALU.mult)
+            nc.vector.tensor_scalar(rb[t][:], low[:], gain[:, t : t + 1], None, ALU.mult)
+            if t == PACK - 1:
+                cand_sc = keep.tile([P, C], U8, name="cand_sc", tag="slot_b3", align_bytes=64)
                 nc.vector.tensor_copy(cand_sc[:], x_sc[:].indirect(cand_l[:]))
                 held["cand_plane"] = keep.tile([P, C], U8, name="cand_plane", align_bytes=64)
                 nc.vector.tensor_copy(held["cand_plane"][:].bitcast(I32), cand_sc[:].bitcast(I32))
-                place_rows(held["cand_plane"], nc.sync)
-            xc_w[t] = keep.tile([P, P], U32, name="xc_w%d" % t, tag="slot_a%d" % t, align_bytes=64)
-            nc.vector.tensor_copy(xc_w[t][:], x_w[:].indirect(cand_l[:, t * P // GROUP : (t + 1) * P // GROUP]))
+                place_rows(held["cand_plane"], (nc.sync, nc.sync, nc.sync))
+
+        def pick_candidates(c, tag):
+            xc_w[c] = keep.tile([P, P], U32, name="xc_w%d" % c, tag=tag, align_bytes=64)
+            nc.vector.tensor_copy(xc_w[c][:], x_w[:].indirect(cand_l[:, c * P // GROUP : (c + 1) * P // GROUP]))
 
         def put_a(t):
-            dt[t] = keep.tile([P, WIDE], F32, name="dt%d" % t)
-            put(dt[t], n1_l[:], weighted[t][:, :W])
+            dt[t] = keep.tile([P, WIDE], F32, name="dt%d" % t, tag={0: "high1", 3: "ra2"}.get(t, "dt%d" % t), align_bytes=64)
+            put(dt[t], n1_l[:], ra[t][:])
+            if t < 2:
+                pick_candidates(t, "ra%d" % t)
 
         def put_b(t):
-            put(dt[t], n2_l[:], weighted[t][:, W:])
+            put(dt[t], n2_l[:], rb[t][:])
+            if t < 2:
+                pick_candidates(t + 2, "rb%d" % t)
 
         def finish_z(t, lo, hi):
-            other = fetch("dt_n3_%d_%d" % (t, lo), dt[t], n3_l[:, lo // GROUP : hi // GROUP])
+            other = fetch("dt_n3_%d_%d" % (t, lo), dt[t], n3_l[:, lo // GROUP : hi // GROUP], "low%d" % (t + 1) if t in (1, 2) else None)
             nc.vector.tensor_tensor(z[:, lo:hi, t], dt[t][:, lo:hi], other[:], ALU.subtract)
             if t == PACK - 1 and hi % (S // 2) == 0:
                 lo = hi - S // 2

@@ -43,7 +43,7 @@ def tile_picked_hpqhorddswapd_none_p_kernel(
             table = keep.tile([P, source.shape[2]], U8, name=name, align_bytes=64)
             rows = source[0].bitcast(I32)
             spread = rows.unsqueeze(1).to_broadcast([rows.shape[0], BLOCK, rows.shape[1]])
-            nc.scalar.dma_start(table[:].bitcast(I32), spread)
+            nc.sync.dma_start(table[:].bitcast(I32), spread)
             return table
 
         def load_word_table(name, source):

from contextlib import ExitStack

import concourse.mybir as mybir

K, T, S, G, H, W, C = 512, 1024, 256, 2048, 512, 128, 512
FLOPS = 2 * K * H * S + 2 * K * C * S

F32 = mybir.dt.float32
BF16 = mybir.dt.bfloat16
I32 = mybir.dt.int32
U32 = mybir.dt.uint32
U16 = mybir.dt.uint16
U8 = mybir.dt.uint8
FP8X4 = mybir.dt.float8_e4m3fn_x4
ALU = mybir.AluOpType
COPY = mybir.ActivationFunctionType.Copy

P = 128
PACK = 4
GROUP = 16
QUAD = 32
BLOCK = 8
WIDE = S + 8
HALVES = ((0, 128), (128, 256))
LAST_PIECES = ((0, 64), (64, 128), (128, 256))


def tile_picked_hpqhorddswapd_none_p_kernel(
    tc, x_words, x_scales, d_words, d_scales, gs, offs, k1, n1, n2, n3, cand, n4, n5, n6, out
):
    nc = tc.nc
    with ExitStack() as ctx:
        lists = ctx.enter_context(tc.tile_pool(name="lists", bufs=1))
        keep = ctx.enter_context(tc.tile_pool(name="keep", bufs=1))
        psum = ctx.enter_context(tc.psum_pool(name="psum", bufs=1))

        def load_list(name, source):
            held = lists.tile([P, source.shape[1]], U16, name=name)
            nc.sync.dma_start(held[:], source)
            return held

        def load_scale_table(name, source):
            table = keep.tile([P, source.shape[2]], U8, name=name, align_bytes=64)
            rows = source[0].bitcast(I32)
            spread = rows.unsqueeze(1).to_broadcast([rows.shape[0], BLOCK, rows.shape[1]])
            nc.sync.dma_start(table[:].bitcast(I32), spread)
            return table

        def load_word_table(name, source):
            table = keep.tile([P, source.shape[2]], U32, name=name, align_bytes=64)
            nc.sync.dma_start(table[:].bitcast(I32), source[0].rearrange("p n t -> p (n t)").bitcast(I32))
            return table

        def place_rows(plane, queues):
            for i in range(1, QUAD // BLOCK):
                queues[i - 1].dma_start(plane[i:P:QUAD, :].bitcast(I32), plane[BLOCK * i : P : QUAD, :].bitcast(I32))

        d_sc = load_scale_table("d_sc", d_scales)
        k1_l = load_list("k1_l", k1)
        x_sc = load_scale_table("x_sc", x_scales)
        offs_l = load_list("offs_l", offs)
        n1_l = load_list("n1_l", n1)
        n2_l = load_list("n2_l", n2)
        n3_l = load_list("n3_l", n3)
        d_w = load_word_table("d_w", d_words)
        x_w = load_word_table("x_w", x_words)
        cand_l = load_list("cand_l", cand)
        n4_l = load_list("n4_l", n4)
        n5_l = load_list("n5_l", n5)
        n6_l = load_list("n6_l", n6)

        first_sc = keep.tile([P, H + S], U8, name="first_sc", align_bytes=64)
        first_plane = keep.tile([P, H + S], U8, name="first_plane", align_bytes=64)
        nc.vector.tensor_copy(first_sc[:, :H], d_sc[:].indirect(k1_l[:]))
        nc.vector.tensor_copy(first_sc[:, H:], x_sc[:].indirect(offs_l[:]))
        nc.vector.tensor_copy(
            first_plane[:, :H].rearrange("p (t m) -> p t m", t=PACK),
            first_sc[:, :H].rearrange("p (m t) -> p t m", t=PACK),
        )
        nc.vector.tensor_copy(first_plane[:, H:].bitcast(I32), first_sc[:, H:].bitcast(I32))
        place_rows(first_plane, (nc.scalar, nc.scalar, nc.scalar))
        dk_w = keep.tile([P, H], U32, name="dk_w", align_bytes=64)
        nc.vector.tensor_copy(dk_w[:], d_w[:].indirect(k1_l[:]))
        xq_w = keep.tile([P, S], U32, name="xq_w", align_bytes=64)
        for lo, hi in HALVES:
            nc.vector.tensor_copy(xq_w[:, lo:hi], x_w[:].indirect(offs_l[:, lo // GROUP : hi // GROUP]))

        h = []
        for t in range(PACK):
            dealt_w = keep.tile([P, P], U32, name="dealt_w%d" % t, align_bytes=64)
            nc.vector.tensor_copy(dealt_w[:], dk_w[:, t:H:PACK])
            h_t = keep.tile([P, S], F32, name="h%d" % t)
            for i, (lo, hi) in enumerate(HALVES if t == 0 else ((0, S),)):
                acc = psum.tile([P, hi - lo], F32, name="acc_h%d_%d" % (t, i), tag="bank%d" % (t + PACK * i))
                nc.tensor.matmul_mx(
                    out=acc[:],
                    lhsT=dealt_w[:].bitcast(FP8X4),
                    lhsT_scale=first_plane[:, t * P : (t + 1) * P],
                    rhs=xq_w[:, lo:hi].bitcast(FP8X4),
                    rhs_scale=first_plane[:, H + lo : H + hi],
                    start=True,
                    stop=True,
                )
                if t == 0 and i == 0:
                    nc.scalar.activation(h_t[:, lo:hi], acc[:], COPY, scale=0.0625)
                else:
                    nc.vector.tensor_scalar(h_t[:, lo:hi], acc[:], 0.0625, None, ALU.mult)
            h.append(h_t)

        gain = keep.tile([P, PACK], F32, name="gain", tag="d_w", align_bytes=64)
        nc.sync.dma_start(gain[:], gs.rearrange("(p t) o -> p (t o)", t=PACK))

        def fetch(name, window, offsets, tag=None):
            got = keep.tile([P, offsets.shape[1] * GROUP], F32, name=name, tag=tag or name, align_bytes=64)
            nc.scalar.activation(got[:], window[:].indirect(offsets), COPY)
            return got

        def put(window, offsets, values):
            nc.scalar.activation(window[:].indirect(offsets), values, COPY)

        z = keep.tile([P, S, PACK], BF16, name="z", align_bytes=64)
        z_w = keep.tile([P, S], U32, name="z_w", align_bytes=64)
        z_sc = keep.tile([P, S], U8, name="z_sc", align_bytes=64)
        pa, pb, ra, rb, dt, xc_w = {}, {}, {}, {}, {}, {}
        held = {}

        def fetch_a(t):
            pa[t] = fetch("pa%d" % t, h[t], n1_l[:])

        def fetch_b(t):
            pb[t] = fetch("pb%d" % t, h[t], n2_l[:], "slot_b%d" % t)
            high = keep.tile([P, W], F32, name="high%d" % t, align_bytes=64)
            low = keep.tile([P, W], F32, name="low%d" % t, align_bytes=64)
            ra[t] = keep.tile([P, W], F32, name="ra%d" % t, align_bytes=64)
            rb[t] = keep.tile([P, W], F32, name="rb%d" % t, align_bytes=64)
            nc.vector.tensor_tensor(high[:], pa[t][:], pb[t][:], ALU.max)
            nc.vector.tensor_tensor(low[:], pa[t][:], pb[t][:], ALU.min)
            nc.vector.tensor_scalar(ra[t][:], high[:], gain[:, t : t + 1], None, ALU.mult)
            nc.vector.tensor_scalar(rb[t][:], low[:], gain[:, t : t + 1], None, ALU.mult)
            if t == PACK - 1:
                cand_sc = keep.tile([P, C], U8, name="cand_sc", tag="slot_b3", align_bytes=64)
                nc.vector.tensor_copy(cand_sc[:], x_sc[:].indirect(cand_l[:]))
                held["cand_plane"] = keep.tile([P, C], U8, name="cand_plane", align_bytes=64)
                nc.vector.tensor_copy(held["cand_plane"][:].bitcast(I32), cand_sc[:].bitcast(I32))
                place_rows(held["cand_plane"], (nc.sync, nc.sync, nc.sync))

        def pick_candidates(c, tag):
            xc_w[c] = keep.tile([P, P], U32, name="xc_w%d" % c, tag=tag, align_bytes=64)
            nc.vector.tensor_copy(xc_w[c][:], x_w[:].indirect(cand_l[:, c * P // GROUP : (c + 1) * P // GROUP]))

        def put_a(t):
            dt[t] = keep.tile([P, WIDE], F32, name="dt%d" % t, tag={0: "high1", 3: "ra2"}.get(t, "dt%d" % t), align_bytes=64)
            put(dt[t], n1_l[:], ra[t][:])
            if t < 2:
                pick_candidates(t, "ra%d" % t)

        def put_b(t):
            put(dt[t], n2_l[:], rb[t][:])
            if t < 2:
                pick_candidates(t + 2, "rb%d" % t)

        def finish_z(t, lo, hi):
            other = fetch("dt_n3_%d_%d" % (t, lo), dt[t], n3_l[:, lo // GROUP : hi // GROUP], "low%d" % (t + 1) if t in (1, 2) else None)
            nc.vector.tensor_tensor(z[:, lo:hi, t], dt[t][:, lo:hi], other[:], ALU.subtract)
            if t == PACK - 1 and hi % (S // 2) == 0:
                lo = hi - S // 2
                nc.vector.quantize_mx(
                    out=z_w[:, lo:hi].bitcast(FP8X4),
                    scales=z_sc[:, lo:hi],
                    in_=z[:, lo:hi, :].rearrange("p n t -> p (n t)"),
                )

        def weave(get_a, get_b, set_a, set_b, finish, before, pieces):
            for b in range(3):
                get_a(b)
                get_b(b)
            set_a(0)
            get_a(3)
            set_b(0)
            get_b(3)
            for b in range(1, 4):
                set_a(b)
                finish(b - 1, 0, S if b < 3 else before)
                set_b(b)
            if before < S:
                finish(2, before, S)
            for lo, hi in pieces:
                finish(3, lo, hi)

        weave(fetch_a, fetch_b, put_a, put_b, finish_z, S, LAST_PIECES)

        s = []
        for c in range(C // P):
            s_c = keep.tile([P, S], F32, name="s%d" % c)
            for i, (lo, hi) in enumerate(HALVES if c == 0 else ((0, S),)):
                acc = psum.tile([P, hi - lo], F32, name="acc_s%d_%d" % (c, i), tag="bank%d" % ((PACK + c + 4 * i) % 8))
                nc.tensor.matmul_mx(
                    out=acc[:],
                    lhsT=xc_w[c][:].bitcast(FP8X4),
                    lhsT_scale=held["cand_plane"][:, c * P : (c + 1) * P],
                    rhs=z_w[:, lo:hi].bitcast(FP8X4),
                    rhs_scale=z_sc[:, lo:hi],
                    start=True,
                    stop=True,
                )
                nc.vector.tensor_scalar(s_c[:, lo:hi], acc[:], 0.0625, None, ALU.mult)
            s.append(s_c)

        pa2, pb2, rb2, dt2 = {}, {}, {}, {}

        def fetch_a2(c):
            pa2[c] = fetch("pa2_%d" % c, s[c], n4_l[:])

        def fetch_b2(c):
            pb2[c] = fetch("pb2_%d" % c, s[c], n5_l[:])
            rb2[c] = keep.tile([P, W], F32, name="rb2_%d" % c)
            nc.vector.tensor_tensor(rb2[c][:], pa2[c][:], pb2[c][:], ALU.subtract)

        def put_a2(c):
            dt2[c] = keep.tile([P, WIDE], F32, name="dt2_%d" % c)
            put(dt2[c], n4_l[:], pb2[c][:])

        def put_b2(c):
            put(dt2[c], n5_l[:], rb2[c][:])

        def finish_out(c, lo, hi):
            other = fetch("dt2_n6_%d_%d" % (c, lo), dt2[c], n6_l[:, lo // GROUP : hi // GROUP])
            result = keep.tile([P, hi - lo], F32, name="result%d_%d" % (c, lo))
            nc.vector.scalar_tensor_tensor(result[:], other[:], 0.5, dt2[c][:, lo:hi], ALU.mult, ALU.max)
            nc.sync.dma_start(out[c * P : (c + 1) * P, lo:hi], result[:])

        weave(fetch_a2, fetch_b2, put_a2, put_b2, finish_out, S // 2, HALVES)
